import numpy as np
import ml_dtypes


def mxq(x, axis, fmt="e4m3"):
    dtype, down = {"e4m3": (ml_dtypes.float8_e4m3fn, 7), "e5m2": (ml_dtypes.float8_e5m2, 14)}[fmt]
    v = np.moveaxis(np.asarray(x, np.float32).astype(ml_dtypes.bfloat16).astype(np.float64), axis, -1)
    blocks = v.reshape(v.shape[:-1] + (-1, 32))
    amax = np.abs(blocks).max(-1, keepdims=True)
    byte = np.maximum(np.where(amax > 0, np.frexp(amax)[1] - 1 + 127, 0) - down, 1)
    scale = np.exp2(byte - 127.0)
    codes = (blocks / scale).astype(np.float32).astype(dtype).astype(np.float64)
    return np.moveaxis((codes * scale).reshape(v.shape), -1, axis)


WIDE = False


def mx_kscale(k):
    if not WIDE:
        return np.ones(k)
    levels = np.array([30, -30])
    if k % 512:
        return np.exp2(np.random.permutation(np.resize(levels, k // 32))).repeat(32)
    a = np.empty((k // 512, 16))
    for p in range(k // 512):
        a[p, :8] = np.random.permutation(np.resize(levels, 8))
        for g in range(8):
            far = levels[np.abs(levels - a[p, g]) >= 10]
            a[p, g + 8] = far[np.random.randint(len(far))]
    return np.exp2(a.ravel()).repeat(32)


def f64(x):
    return np.asarray(x).astype(np.float64)


def striped(idx):
    return np.tile(np.asarray(idx).reshape(-1, 16).T, (8, 1)).astype(np.uint16)


def unstriped(offs):
    return offs[:16].T.reshape(-1).astype(np.int64)


def bf(x):
    return np.asarray(x, np.float32).astype(ml_dtypes.bfloat16)


def planes(Y):
    r, m = Y.shape
    b = f64(bf(Y)).reshape(r // 32, 32, m)
    amax = np.abs(b).max(1)
    byte = np.clip(np.where(amax > 0, np.frexp(amax)[1] - 1 + 127 - 7, 1), 1, 254)
    codes = (b * np.exp2(127.0 - byte)[:, None, :]).reshape(r, m).astype(np.float32).astype(ml_dtypes.float8_e4m3fn).view(np.uint8)
    words = codes.reshape(r // 512, 128, 4, m).transpose(0, 1, 3, 2)
    return np.ascontiguousarray(words), np.ascontiguousarray(byte.astype(np.uint8).reshape(r // 512, 16, m))


K, T, J, N, I = 512, 2048, 512, 2048, 512


def setup_inputs():
    n = np.random.standard_normal
    idx = np.random.permutation(T)[:J]
    idx2 = np.random.permutation(N)[:I]
    fj = mx_kscale(J)
    tj = np.ones(T)
    tj[idx] = fj
    return {
        "xt": (n((K, T)) * tj).astype(np.float32),
        "gj": (n((J, N)) * np.exp(0.5 * n((J, 1))) / fj[:, None]).astype(np.float32),
        "mom": (1.0 * n((K, N))).astype(np.float32),
        "offs": striped(idx),
        "offs2": striped(idx2),
    }


def reference(xt, gj, mom, offs, offs2):
    idx = unstriped(offs)
    idx2 = unstriped(offs2)
    xj = f64(xt)[:, idx].T
    xjq = mxq(xj, 0, "e4m3")
    gjidx2q = mxq(f64(gj)[:, idx2], 0, "e5m2")
    w = xjq.T @ gjidx2q
    d = 0.04 * w + 0.9 * f64(mom)[:, idx2]
    y = np.tanh(d)
    words, scales = planes(y)
    return y, words, scales

@@ -1,0 +1,144 @@
+from contextlib import ExitStack
+
+import concourse.mybir as mybir
+from concourse.masks import make_identity
+
+K, T, J, N, I = 512, 2048, 512, 2048, 512
+FLOPS = 2 * K * J * I
+
+F32 = mybir.dt.float32
+BF16 = mybir.dt.bfloat16
+U32 = mybir.dt.uint32
+U16 = mybir.dt.uint16
+I32 = mybir.dt.int32
+U8 = mybir.dt.uint8
+E4M3X4 = mybir.dt.float8_e4m3fn_x4
+E5M2X4 = mybir.dt.float8_e5m2_x4
+ACT = mybir.ActivationFunctionType
+ALU = mybir.AluOpType
+
+P = 128
+PACK = 4
+PER_COL = 16
+W_GAIN = 0.04
+MOM_GAIN = 0.9
+HALF = I // 2
+
+
+def tile_list_wgrad_lists_on_both_sides_pl_kernel(tc, xt, gj, mom, offs, offs2, out_0, out_1, out_2):
+    nc = tc.nc
+    with ExitStack() as ctx:
+        lists = ctx.enter_context(tc.tile_pool(name="lists", bufs=1))
+        keep = ctx.enter_context(tc.tile_pool(name="keep", bufs=1))
+        psum = ctx.enter_context(tc.psum_pool(name="psum", bufs=1))
+
+        tok_list = lists.tile([P, J // PER_COL], U16, name="tok_list")
+        feat_list = lists.tile([P, I // PER_COL], U16, name="feat_list")
+
+        xt_rows = xt.rearrange("(p t) c -> p t c", t=PACK)
+        gj_rows = gj.rearrange("(p t) c -> p t c", t=PACK)
+        mom_rows = mom.rearrange("(p t) c -> p t c", t=PACK)
+        y_rows = out_0.rearrange("(p t) c -> p t c", t=PACK)
+
+        g_win = [keep.tile([P, N], F32, name=f"g_win{t}") for t in range(PACK)]
+        x_win = [keep.tile([P, T], F32, name=f"x_win{t}") for t in range(PACK)]
+        m_win = [keep.tile([P, N], F32, name=f"m_win{t}") for t in range(PACK)]
+
+        nc.sync.dma_start(g_win[0][:], gj_rows[:, 0, :])
+        nc.sync.dma_start(feat_list[:], offs2)
+        nc.sync.dma_start(tok_list[:], offs)
+        for t in range(1, PACK):
+            nc.sync.dma_start(g_win[t][:], gj_rows[:, t, :])
+        for t in range(PACK):
+            nc.sync.dma_start(x_win[t][:], xt_rows[:, t, :])
+        for t in range(PACK):
+            nc.sync.dma_start(m_win[t][:], mom_rows[:, t, :])
+
+        ident = keep.tile([P, P], F32, name="ident")
+        make_identity(nc, ident[:])
+
+        g_grp = keep.tile([P, I, PACK], BF16, name="g_grp", align_bytes=64)
+        for t in range(PACK):
+            nc.vector.tensor_copy(g_grp[:, :, t], g_win[t][:].indirect(feat_list[:]))
+        g_codes = keep.tile([P, I], U32, name="g_codes", align_bytes=64)
+        g_scales = keep.tile([P, I], U8, name="g_scales", align_bytes=64)
+        nc.vector.quantize_mx(
+            out=g_codes[:].bitcast(E5M2X4),
+            scales=g_scales[:],
+            in_=g_grp[:].rearrange("p c t -> p (c t)"),
+        )
+
+        w_bank = []
+        w_sb = []
+        for t in range(PACK):
+            x_pick = keep.tile([P, J], BF16, name=f"x_pick{t}")
+            nc.scalar.activation(x_pick[:], x_win[t][:].indirect(tok_list[:]), ACT.Copy)
+            words = x_pick[:].bitcast(F32)
+            turned = psum.tile([P, 2, P], F32, name=f"turned{t}")
+            for u in range(2):
+                nc.tensor.transpose(turned[:, u, :], words[:, u : J // 2 : 2], ident[:])
+            x_grp = keep.tile([P, P * PACK], BF16, name=f"x_grp{t}", align_bytes=64)
+            nc.vector.tensor_copy(
+                x_grp[:].bitcast(F32).rearrange("p (q u) -> p q u", u=2),
+                turned[:].rearrange("p u q -> p q u"),
+            )
+            x_codes = keep.tile([P, P], U32, name=f"x_codes{t}", align_bytes=64)
+            x_scales = keep.tile([P, P], U8, name=f"x_scales{t}", align_bytes=64)
+            nc.vector.quantize_mx(out=x_codes[:].bitcast(E4M3X4), scales=x_scales[:], in_=x_grp[:])
+            acc = psum.tile([P, I], F32, name=f"acc{t}")
+            nc.tensor.matmul_mx(
+                out=acc[:],
+                lhsT=x_codes[:].bitcast(E4M3X4),
+                lhsT_scale=x_scales[:],
+                rhs=g_codes[:].bitcast(E5M2X4),
+                rhs_scale=g_scales[:],
+                start=True,
+                stop=True,
+            )
+            scaled = keep.tile([P, I], F32, name=f"w_scaled{t}")
+            nc.scalar.activation(scaled[:], acc[:], ACT.Copy, scale=W_GAIN / MOM_GAIN)
+            w_bank.append(acc)
+            w_sb.append(scaled)
+
+        y = keep.tile([P, PACK, I], F32, name="y")
+        y_grp = [keep.tile([P, HALF, PACK], BF16, name=f"y_grp{h}", align_bytes=64) for h in range(2)]
+        y_codes = keep.tile([P, I], U32, name="y_codes", align_bytes=64)
+        y_scales = keep.tile([P, I], U8, name="y_scales", align_bytes=64)
+        words_out = out_1[0].rearrange("p c r -> p (c r)").bitcast(I32)
+        scales_out = out_2[0].bitcast(I32)
+
+        def cols(h):
+            return slice(h * HALF, (h + 1) * HALF)
+
+        def offsets(h):
+            return feat_list[:, h * HALF // PER_COL : (h + 1) * HALF // PER_COL]
+
+        for t in range(PACK):
+            d0 = keep.tile([P, HALF], F32, name=f"d0_{t}")
+            nc.vector.tensor_tensor(d0[:], m_win[t][:].indirect(offsets(0)), w_sb[t][:, cols(0)], ALU.add)
+            m_pick = keep.tile([P, HALF], F32, name=f"m_pick{t}")
+            nc.scalar.activation(m_pick[:], m_win[t][:].indirect(offsets(1)), ACT.Copy)
+            d1 = keep.tile([P, HALF], F32, name=f"d1_{t}")
+            nc.vector.tensor_tensor(d1[:], m_pick[:], w_sb[t][:, cols(1)], ALU.add)
+            nc.scalar.activation(y[:, t, cols(0)], d0[:], ACT.Tanh, scale=MOM_GAIN)
+            nc.scalar.activation(y[:, t, cols(1)], d1[:], ACT.Tanh, scale=MOM_GAIN)
+            if t == PACK - 2:
+                nc.sync.dma_start(y_rows[:, 0 : PACK - 1, :], y[:, 0 : PACK - 1, :])
+            if t == PACK - 1:
+                nc.sync.dma_start(y_rows[:, t, :], y[:, t, :])
+            if t % 2 == 1:
+                for h in range(2):
+                    nc.vector.tensor_copy(
+                        y_grp[h][:, :, t - 1 : t + 1],
+                        y[:, t - 1 : t + 1, cols(h)].rearrange("p t c -> p c t"),
+                    )
+        for h in range(2):
+            nc.vector.quantize_mx(
+                out=y_codes[:, cols(h)].bitcast(E4M3X4),
+                scales=y_scales[:, cols(h)],
+                in_=y_grp[h][:].rearrange("p c t -> p (c t)"),
+            )
+            nc.sync.dma_start(words_out[:, cols(h)], y_codes[:, cols(h)].bitcast(I32))
+        for q in range(4):
+            queue = nc.scalar if q % 2 == 0 else nc.sync
+            queue.dma_start(scales_out[4 * q : 4 * q + 4, :], y_scales[32 * q : 32 * q + 4, :].bitcast(I32))

@@ -23,6 +23,8 @@ PER_COL = 16
 W_GAIN = 0.04
 MOM_GAIN = 0.9
 HALF = I // 2
+CHUNKS = 4
+CHUNK = I // CHUNKS
 
 
 def tile_list_wgrad_lists_on_both_sides_pl_kernel(tc, xt, gj, mom, offs, offs2, out_0, out_1, out_2):
@@ -44,32 +46,20 @@ def tile_list_wgrad_lists_on_both_sides_pl_kernel(tc, xt, gj, mom, offs, offs2, 
         x_win = [keep.tile([P, T], F32, name=f"x_win{t}") for t in range(PACK)]
         m_win = [keep.tile([P, N], F32, name=f"m_win{t}") for t in range(PACK)]
 
-        nc.sync.dma_start(g_win[0][:], gj_rows[:, 0, :])
-        nc.sync.dma_start(feat_list[:], offs2)
+        nc.sync.dma_start(x_win[0][:], xt_rows[:, 0, :])
         nc.sync.dma_start(tok_list[:], offs)
+        nc.sync.dma_start(feat_list[:], offs2)
         for t in range(1, PACK):
-            nc.sync.dma_start(g_win[t][:], gj_rows[:, t, :])
-        for t in range(PACK):
             nc.sync.dma_start(x_win[t][:], xt_rows[:, t, :])
+        for t in range(PACK):
+            nc.sync.dma_start(g_win[t][:], gj_rows[:, t, :])
         for t in range(PACK):
             nc.sync.dma_start(m_win[t][:], mom_rows[:, t, :])
 
         ident = keep.tile([P, P], F32, name="ident")
         make_identity(nc, ident[:])
 
-        g_grp = keep.tile([P, I, PACK], BF16, name="g_grp", align_bytes=64)
-        for t in range(PACK):
-            nc.vector.tensor_copy(g_grp[:, :, t], g_win[t][:].indirect(feat_list[:]))
-        g_codes = keep.tile([P, I], U32, name="g_codes", align_bytes=64)
-        g_scales = keep.tile([P, I], U8, name="g_scales", align_bytes=64)
-        nc.vector.quantize_mx(
-            out=g_codes[:].bitcast(E5M2X4),
-            scales=g_scales[:],
-            in_=g_grp[:].rearrange("p c t -> p (c t)"),
-        )
-
-        w_bank = []
-        w_sb = []
+        x_ops = []
         for t in range(PACK):
             x_pick = keep.tile([P, J], BF16, name=f"x_pick{t}")
             nc.scalar.activation(x_pick[:], x_win[t][:].indirect(tok_list[:]), ACT.Copy)
@@ -85,6 +75,22 @@ def tile_list_wgrad_lists_on_both_sides_pl_kernel(tc, xt, gj, mom, offs, offs2, 
             x_codes = keep.tile([P, P], U32, name=f"x_codes{t}", align_bytes=64)
             x_scales = keep.tile([P, P], U8, name=f"x_scales{t}", align_bytes=64)
             nc.vector.quantize_mx(out=x_codes[:].bitcast(E4M3X4), scales=x_scales[:], in_=x_grp[:])
+            x_ops.append((x_codes, x_scales))
+
+        g_grp = keep.tile([P, I, PACK], BF16, name="g_grp", align_bytes=64)
+        for t in range(PACK):
+            nc.vector.tensor_copy(g_grp[:, :, t], g_win[t][:].indirect(feat_list[:]))
+        g_codes = keep.tile([P, I], U32, name="g_codes", align_bytes=64)
+        g_scales = keep.tile([P, I], U8, name="g_scales", align_bytes=64)
+        nc.vector.quantize_mx(
+            out=g_codes[:].bitcast(E5M2X4),
+            scales=g_scales[:],
+            in_=g_grp[:].rearrange("p c t -> p (c t)"),
+        )
+
+        w_bank = []
+        for t in range(PACK):
+            x_codes, x_scales = x_ops[t]
             acc = psum.tile([P, I], F32, name=f"acc{t}")
             nc.tensor.matmul_mx(
                 out=acc[:],
@@ -95,50 +101,59 @@ def tile_list_wgrad_lists_on_both_sides_pl_kernel(tc, xt, gj, mom, offs, offs2, 
                 start=True,
                 stop=True,
             )
-            scaled = keep.tile([P, I], F32, name=f"w_scaled{t}")
-            nc.scalar.activation(scaled[:], acc[:], ACT.Copy, scale=W_GAIN / MOM_GAIN)
             w_bank.append(acc)
-            w_sb.append(scaled)
 
         y = keep.tile([P, PACK, I], F32, name="y")
-        y_grp = [keep.tile([P, HALF, PACK], BF16, name=f"y_grp{h}", align_bytes=64) for h in range(2)]
         y_codes = keep.tile([P, I], U32, name="y_codes", align_bytes=64)
         y_scales = keep.tile([P, I], U8, name="y_scales", align_bytes=64)
         words_out = out_1[0].rearrange("p c r -> p (c r)").bitcast(I32)
         scales_out = out_2[0].bitcast(I32)
 
-        def cols(h):
-            return slice(h * HALF, (h + 1) * HALF)
+        def cols(c, width=CHUNK):
+            return slice(c * width, (c + 1) * width)
 
-        def offsets(h):
-            return feat_list[:, h * HALF // PER_COL : (h + 1) * HALF // PER_COL]
+        def finish_rows(t):
+            picks = []
+            for c in range(CHUNKS):
+                pick = keep.tile([P, CHUNK], F32, name=f"pick{t}_{c}", tag=f"ring{t % 2}_{c}", align_bytes=64)
+                listed = m_win[t][:].indirect(feat_list[:, cols(c, CHUNK // PER_COL)])
+                if c % 2 == 0:
+                    nc.vector.tensor_copy(pick[:], listed)
+                else:
+                    nc.scalar.activation(pick[:], listed, ACT.Copy)
+                picks.append(pick)
+            for c in range(CHUNKS):
+                tag = f"ring{(t + 1) % 2}_{c}" if t < PACK - 1 else f"last_{c}"
+                d = keep.tile([P, CHUNK], F32, name=f"d{t}_{c}", tag=tag, align_bytes=64)
+                nc.vector.scalar_tensor_tensor(
+                    d[:], w_bank[t][:, cols(c)], W_GAIN / MOM_GAIN, picks[c][:], ALU.mult, ALU.add
+                )
+                nc.scalar.activation(y[:, t, cols(c)], d[:], ACT.Tanh, scale=MOM_GAIN)
 
-        for t in range(PACK):
-            d0 = keep.tile([P, HALF], F32, name=f"d0_{t}")
-            nc.vector.tensor_tensor(d0[:], m_win[t][:].indirect(offsets(0)), w_sb[t][:, cols(0)], ALU.add)
-            m_pick = keep.tile([P, HALF], F32, name=f"m_pick{t}")
-            nc.scalar.activation(m_pick[:], m_win[t][:].indirect(offsets(1)), ACT.Copy)
-            d1 = keep.tile([P, HALF], F32, name=f"d1_{t}")
-            nc.vector.tensor_tensor(d1[:], m_pick[:], w_sb[t][:, cols(1)], ALU.add)
-            nc.scalar.activation(y[:, t, cols(0)], d0[:], ACT.Tanh, scale=MOM_GAIN)
-            nc.scalar.activation(y[:, t, cols(1)], d1[:], ACT.Tanh, scale=MOM_GAIN)
-            if t == PACK - 2:
-                nc.sync.dma_start(y_rows[:, 0 : PACK - 1, :], y[:, 0 : PACK - 1, :])
-            if t == PACK - 1:
-                nc.sync.dma_start(y_rows[:, t, :], y[:, t, :])
-            if t % 2 == 1:
-                for h in range(2):
-                    nc.vector.tensor_copy(
-                        y_grp[h][:, :, t - 1 : t + 1],
-                        y[:, t - 1 : t + 1, cols(h)].rearrange("p t c -> p c t"),
-                    )
+        def round_pair(copy, dst, first, columns):
+            copy(dst[:, :, first : first + 2], y[:, first : first + 2, columns].rearrange("p t c -> p c t"))
+
+        for t in range(PACK - 1):
+            finish_rows(t)
+        nc.sync.dma_start(y_rows[:, 0 : PACK - 1, :], y[:, 0 : PACK - 1, :])
+        y_grp = [
+            keep.tile([P, HALF, PACK], BF16, name=f"y_grp{h}", tag=f"ring0_{2 * h + 1}", align_bytes=64)
+            for h in range(2)
+        ]
+        for h in range(2):
+            round_pair(nc.vector.tensor_copy, y_grp[h][:], 0, cols(h, HALF))
+        finish_rows(PACK - 1)
+        nc.sync.dma_start(y_rows[:, PACK - 1, :], y[:, PACK - 1, :])
+        round_pair(nc.vector.tensor_copy, y_grp[0][:], 2, cols(0, HALF))
+        round_pair(nc.vector.tensor_copy, y_grp[1][:, 0:CHUNK, :], 2, cols(2))
+        round_pair(nc.scalar.copy, y_grp[1][:, CHUNK:HALF, :], 2, cols(3))
         for h in range(2):
             nc.vector.quantize_mx(
-                out=y_codes[:, cols(h)].bitcast(E4M3X4),
-                scales=y_scales[:, cols(h)],
+                out=y_codes[:, cols(h, HALF)].bitcast(E4M3X4),
+                scales=y_scales[:, cols(h, HALF)],
                 in_=y_grp[h][:].rearrange("p c t -> p (c t)"),
             )
-            nc.sync.dma_start(words_out[:, cols(h)], y_codes[:, cols(h)].bitcast(I32))
+            nc.sync.dma_start(words_out[:, cols(h, HALF)], y_codes[:, cols(h, HALF)].bitcast(I32))
         for q in range(4):
             queue = nc.scalar if q % 2 == 0 else nc.sync
             queue.dma_start(scales_out[4 * q : 4 * q + 4, :], y_scales[32 * q : 32 * q + 4, :].bitcast(I32))

@@ -42,44 +42,56 @@ def tile_list_wgrad_lists_on_both_sides_pl_kernel(tc, xt, gj, mom, offs, offs2, 
         mom_rows = mom.rearrange("(p t) c -> p t c", t=PACK)
         y_rows = out_0.rearrange("(p t) c -> p t c", t=PACK)
 
-        g_win = [keep.tile([P, N], F32, name=f"g_win{t}") for t in range(PACK)]
-        x_win = [keep.tile([P, T], F32, name=f"x_win{t}") for t in range(PACK)]
+        x_two = [keep.tile([P, 2, T], F32, name=f"x_two{a}") for a in range(2)]
+        g_two = keep.tile([P, 2, N], F32, name="g_two")
+        g_one = [keep.tile([P, N], F32, name=f"g_one{t}") for t in range(2, PACK)]
+        g_win = [g_two[:, 0, :], g_two[:, 1, :], g_one[0][:], g_one[1][:]]
         m_win = [keep.tile([P, N], F32, name=f"m_win{t}") for t in range(PACK)]
 
-        nc.sync.dma_start(x_win[0][:], xt_rows[:, 0, :])
+        nc.sync.dma_start(x_two[0][:], xt_rows[:, 0:2, :])
         nc.sync.dma_start(tok_list[:], offs)
         nc.sync.dma_start(feat_list[:], offs2)
-        for t in range(1, PACK):
-            nc.sync.dma_start(x_win[t][:], xt_rows[:, t, :])
-        for t in range(PACK):
-            nc.sync.dma_start(g_win[t][:], gj_rows[:, t, :])
+        nc.sync.dma_start(x_two[1][:], xt_rows[:, 2:4, :])
+        nc.sync.dma_start(g_two[:], gj_rows[:, 0:2, :])
+        for t in range(2, PACK):
+            nc.sync.dma_start(g_win[t], gj_rows[:, t, :])
         for t in range(PACK):
             nc.sync.dma_start(m_win[t][:], mom_rows[:, t, :])
 
         ident = keep.tile([P, P], F32, name="ident")
         make_identity(nc, ident[:])
 
+        def gather(on_vector, dst, listed):
+            if on_vector:
+                nc.vector.tensor_copy(dst, listed)
+            else:
+                nc.scalar.activation(dst, listed, ACT.Copy)
+
         x_ops = []
         for t in range(PACK):
-            x_pick = keep.tile([P, J], BF16, name=f"x_pick{t}")
-            nc.scalar.activation(x_pick[:], x_win[t][:].indirect(tok_list[:]), ACT.Copy)
-            words = x_pick[:].bitcast(F32)
-            turned = psum.tile([P, 2, P], F32, name=f"turned{t}")
-            for u in range(2):
-                nc.tensor.transpose(turned[:, u, :], words[:, u : J // 2 : 2], ident[:])
-            x_grp = keep.tile([P, P * PACK], BF16, name=f"x_grp{t}", align_bytes=64)
-            nc.vector.tensor_copy(
-                x_grp[:].bitcast(F32).rearrange("p (q u) -> p q u", u=2),
-                turned[:].rearrange("p u q -> p q u"),
-            )
+            x_pick = keep.tile([P, J], F32, name=f"x_pick{t}")
+            gather(t % 2 == 0, x_pick[:], x_two[t // 2][:, t % 2, :].indirect(tok_list[:]))
+            turned = psum.tile([P, PACK, P], F32, name=f"turned{t}")
+            for e in range(PACK):
+                nc.tensor.transpose(turned[:, e, :], x_pick[:, e:J:PACK], ident[:])
+            x_grp = keep.tile([P, P, PACK], BF16, name=f"x_grp{t}", align_bytes=64)
+            nc.vector.tensor_copy(x_grp[:], turned[:].rearrange("p e q -> p q e"))
             x_codes = keep.tile([P, P], U32, name=f"x_codes{t}", align_bytes=64)
             x_scales = keep.tile([P, P], U8, name=f"x_scales{t}", align_bytes=64)
-            nc.vector.quantize_mx(out=x_codes[:].bitcast(E4M3X4), scales=x_scales[:], in_=x_grp[:])
+            nc.vector.quantize_mx(
+                out=x_codes[:].bitcast(E4M3X4),
+                scales=x_scales[:],
+                in_=x_grp[:].rearrange("p q e -> p (q e)"),
+            )
             x_ops.append((x_codes, x_scales))
 
         g_grp = keep.tile([P, I, PACK], BF16, name="g_grp", align_bytes=64)
-        for t in range(PACK):
-            nc.vector.tensor_copy(g_grp[:, :, t], g_win[t][:].indirect(feat_list[:]))
+        g_pick = keep.tile([P, I], F32, name="g_pick")
+        nc.scalar.activation(g_pick[:], g_win[1].indirect(feat_list[:]), ACT.Copy)
+        nc.vector.tensor_copy(g_grp[:, :, 0], g_win[0].indirect(feat_list[:]))
+        nc.vector.tensor_copy(g_grp[:, :, 1], g_pick[:])
+        for t in range(2, PACK):
+            nc.vector.tensor_copy(g_grp[:, :, t], g_win[t].indirect(feat_list[:]))
         g_codes = keep.tile([P, I], U32, name="g_codes", align_bytes=64)
         g_scales = keep.tile([P, I], U8, name="g_scales", align_bytes=64)
         nc.vector.quantize_mx(
@@ -112,41 +124,57 @@ def tile_list_wgrad_lists_on_both_sides_pl_kernel(tc, xt, gj, mom, offs, offs2, 
         def cols(c, width=CHUNK):
             return slice(c * width, (c + 1) * width)
 
-        def finish_rows(t):
-            picks = []
-            for c in range(CHUNKS):
-                pick = keep.tile([P, CHUNK], F32, name=f"pick{t}_{c}", tag=f"ring{t % 2}_{c}", align_bytes=64)
-                listed = m_win[t][:].indirect(feat_list[:, cols(c, CHUNK // PER_COL)])
-                if c % 2 == 0:
-                    nc.vector.tensor_copy(pick[:], listed)
-                else:
-                    nc.scalar.activation(pick[:], listed, ACT.Copy)
-                picks.append(pick)
-            for c in range(CHUNKS):
-                tag = f"ring{(t + 1) % 2}_{c}" if t < PACK - 1 else f"last_{c}"
-                d = keep.tile([P, CHUNK], F32, name=f"d{t}_{c}", tag=tag, align_bytes=64)
-                nc.vector.scalar_tensor_tensor(
-                    d[:], w_bank[t][:, cols(c)], W_GAIN / MOM_GAIN, picks[c][:], ALU.mult, ALU.add
-                )
-                nc.scalar.activation(y[:, t, cols(c)], d[:], ACT.Tanh, scale=MOM_GAIN)
+        def listed_mom(t, c):
+            return m_win[t][:].indirect(feat_list[:, cols(c, CHUNK // PER_COL)])
 
-        def round_pair(copy, dst, first, columns):
-            copy(dst[:, :, first : first + 2], y[:, first : first + 2, columns].rearrange("p t c -> p c t"))
+        def add_product(d, t, c, pick):
+            nc.vector.scalar_tensor_tensor(
+                d[:, cols(c)], w_bank[t][:, cols(c)], W_GAIN / MOM_GAIN, pick[:, cols(c)], ALU.mult, ALU.add
+            )
 
-        for t in range(PACK - 1):
-            finish_rows(t)
-        nc.sync.dma_start(y_rows[:, 0 : PACK - 1, :], y[:, 0 : PACK - 1, :])
-        y_grp = [
-            keep.tile([P, HALF, PACK], BF16, name=f"y_grp{h}", tag=f"ring0_{2 * h + 1}", align_bytes=64)
-            for h in range(2)
-        ]
-        for h in range(2):
-            round_pair(nc.vector.tensor_copy, y_grp[h][:], 0, cols(h, HALF))
-        finish_rows(PACK - 1)
-        nc.sync.dma_start(y_rows[:, PACK - 1, :], y[:, PACK - 1, :])
-        round_pair(nc.vector.tensor_copy, y_grp[0][:], 2, cols(0, HALF))
-        round_pair(nc.vector.tensor_copy, y_grp[1][:, 0:CHUNK, :], 2, cols(2))
-        round_pair(nc.scalar.copy, y_grp[1][:, CHUNK:HALF, :], 2, cols(3))
+        def squash(d, t, c):
+            nc.scalar.activation(y[:, t, cols(c)], d[:, cols(c)], ACT.Tanh, scale=MOM_GAIN)
+
+        def finish_rows(t, vector_chunks):
+            pick = keep.tile([P, I], F32, name=f"pick{t}")
+            for c in range(CHUNKS):
+                gather(c in vector_chunks, pick[:, cols(c)], listed_mom(t, c))
+            d = keep.tile([P, I], F32, name=f"d{t}", tag=f"d{t}")
+            for c in range(CHUNKS):
+                add_product(d, t, c, pick)
+                squash(d, t, c)
+
+        def round_pair(copy, first, c):
+            copy(
+                y_grp[c // 2][:, cols(c % 2), first : first + 2],
+                y[:, first : first + 2, cols(c)].rearrange("p t c -> p c t"),
+            )
+
+        y_grp = [keep.tile([P, HALF, PACK], BF16, name=f"y_grp{h}", align_bytes=64) for h in range(2)]
+        for t in range(2):
+            finish_rows(t, (0, 2))
+        nc.sync.dma_start(y_rows[:, 0:2, :], y[:, 0:2, :])
+        for c in range(CHUNKS):
+            round_pair(nc.vector.tensor_copy, 0, c)
+        last = PACK - 1
+        w_last = keep.tile([P, HALF], F32, name="w_last", tag="d1")
+        nc.vector.tensor_scalar_mul(w_last[:], w_bank[last][:, 0:HALF], W_GAIN / MOM_GAIN)
+        finish_rows(2, (3,))
+        nc.sync.dma_start(y_rows[:, 2, :], y[:, 2, :])
+
+        d = keep.tile([P, I], F32, name="d_last")
+        pick = keep.tile([P, I], F32, name="pick_last")
+        for c in range(2):
+            nc.vector.tensor_tensor(d[:, cols(c)], listed_mom(last, c), w_last[:, cols(c)], ALU.add)
+        for c in range(2, CHUNKS):
+            gather(False, pick[:, cols(c)], listed_mom(last, c))
+        for c in range(2, CHUNKS):
+            add_product(d, last, c, pick)
+        for c in range(CHUNKS):
+            squash(d, last, c)
+        nc.sync.dma_start(y_rows[:, last, :], y[:, last, :])
+        for c in range(CHUNKS):
+            round_pair(nc.vector.tensor_copy if c < CHUNKS - 1 else nc.scalar.copy, 2, c)
         for h in range(2):
             nc.vector.quantize_mx(
                 out=y_codes[:, cols(h, HALF)].bitcast(E4M3X4),

@@ -42,24 +42,24 @@ def tile_list_wgrad_lists_on_both_sides_pl_kernel(tc, xt, gj, mom, offs, offs2, 
         mom_rows = mom.rearrange("(p t) c -> p t c", t=PACK)
         y_rows = out_0.rearrange("(p t) c -> p t c", t=PACK)
 
-        x_two = [keep.tile([P, 2, T], F32, name=f"x_two{a}") for a in range(2)]
-        g_two = keep.tile([P, 2, N], F32, name="g_two")
-        g_one = [keep.tile([P, N], F32, name=f"g_one{t}") for t in range(2, PACK)]
-        g_win = [g_two[:, 0, :], g_two[:, 1, :], g_one[0][:], g_one[1][:]]
+        g_two = [keep.tile([P, 2, N], F32, name=f"g_two{a}") for a in range(2)]
+        x_win = [keep.tile([P, T], F32, name=f"x_win{t}") for t in range(PACK)]
         m_win = [keep.tile([P, N], F32, name=f"m_win{t}") for t in range(PACK)]
 
-        nc.sync.dma_start(x_two[0][:], xt_rows[:, 0:2, :])
-        nc.sync.dma_start(tok_list[:], offs)
+        nc.sync.dma_start(g_two[0][:], gj_rows[:, 0:2, :])
         nc.sync.dma_start(feat_list[:], offs2)
-        nc.sync.dma_start(x_two[1][:], xt_rows[:, 2:4, :])
-        nc.sync.dma_start(g_two[:], gj_rows[:, 0:2, :])
-        for t in range(2, PACK):
-            nc.sync.dma_start(g_win[t], gj_rows[:, t, :])
+        nc.sync.dma_start(tok_list[:], offs)
+        nc.sync.dma_start(g_two[1][:], gj_rows[:, 2:4, :])
+        for t in range(PACK):
+            nc.sync.dma_start(x_win[t][:], xt_rows[:, t, :])
         for t in range(PACK):
             nc.sync.dma_start(m_win[t][:], mom_rows[:, t, :])
 
         ident = keep.tile([P, P], F32, name="ident")
         make_identity(nc, ident[:])
+
+        def cols(c, width=CHUNK):
+            return slice(c * width, (c + 1) * width)
 
         def gather(on_vector, dst, listed):
             if on_vector:
@@ -67,31 +67,12 @@ def tile_list_wgrad_lists_on_both_sides_pl_kernel(tc, xt, gj, mom, offs, offs2, 
             else:
                 nc.scalar.activation(dst, listed, ACT.Copy)
 
-        x_ops = []
-        for t in range(PACK):
-            x_pick = keep.tile([P, J], F32, name=f"x_pick{t}")
-            gather(t % 2 == 0, x_pick[:], x_two[t // 2][:, t % 2, :].indirect(tok_list[:]))
-            turned = psum.tile([P, PACK, P], F32, name=f"turned{t}")
-            for e in range(PACK):
-                nc.tensor.transpose(turned[:, e, :], x_pick[:, e:J:PACK], ident[:])
-            x_grp = keep.tile([P, P, PACK], BF16, name=f"x_grp{t}", align_bytes=64)
-            nc.vector.tensor_copy(x_grp[:], turned[:].rearrange("p e q -> p q e"))
-            x_codes = keep.tile([P, P], U32, name=f"x_codes{t}", align_bytes=64)
-            x_scales = keep.tile([P, P], U8, name=f"x_scales{t}", align_bytes=64)
-            nc.vector.quantize_mx(
-                out=x_codes[:].bitcast(E4M3X4),
-                scales=x_scales[:],
-                in_=x_grp[:].rearrange("p q e -> p (q e)"),
-            )
-            x_ops.append((x_codes, x_scales))
-
         g_grp = keep.tile([P, I, PACK], BF16, name="g_grp", align_bytes=64)
-        g_pick = keep.tile([P, I], F32, name="g_pick")
-        nc.scalar.activation(g_pick[:], g_win[1].indirect(feat_list[:]), ACT.Copy)
-        nc.vector.tensor_copy(g_grp[:, :, 0], g_win[0].indirect(feat_list[:]))
-        nc.vector.tensor_copy(g_grp[:, :, 1], g_pick[:])
-        for t in range(2, PACK):
-            nc.vector.tensor_copy(g_grp[:, :, t], g_win[t].indirect(feat_list[:]))
+        for a in range(2):
+            g_pick = keep.tile([P, I], F32, name=f"g_pick{a}")
+            nc.scalar.activation(g_pick[:], g_two[a][:, 1, :].indirect(feat_list[:]), ACT.Copy)
+            nc.vector.tensor_copy(g_grp[:, :, 2 * a], g_two[a][:, 0, :].indirect(feat_list[:]))
+            nc.vector.tensor_copy(g_grp[:, :, 2 * a + 1], g_pick[:])
         g_codes = keep.tile([P, I], U32, name="g_codes", align_bytes=64)
         g_scales = keep.tile([P, I], U8, name="g_scales", align_bytes=64)
         nc.vector.quantize_mx(
@@ -100,9 +81,21 @@ def tile_list_wgrad_lists_on_both_sides_pl_kernel(tc, xt, gj, mom, offs, offs2, 
             in_=g_grp[:].rearrange("p c t -> p (c t)"),
         )
 
-        w_bank = []
-        for t in range(PACK):
-            x_codes, x_scales = x_ops[t]
+        def product(t):
+            x_pick = keep.tile([P, J], BF16, name=f"x_pick{t}")
+            nc.scalar.activation(x_pick[:], x_win[t][:].indirect(tok_list[:]), ACT.Copy)
+            words = x_pick[:].bitcast(F32)
+            turned = psum.tile([P, 2, P], F32, name=f"turned{t}")
+            for u in range(2):
+                nc.tensor.transpose(turned[:, u, :], words[:, u : J // 2 : 2], ident[:])
+            x_grp = keep.tile([P, P * PACK], BF16, name=f"x_grp{t}", align_bytes=64)
+            nc.vector.tensor_copy(
+                x_grp[:].bitcast(F32).rearrange("p (q u) -> p q u", u=2),
+                turned[:].rearrange("p u q -> p q u"),
+            )
+            x_codes = keep.tile([P, P], U32, name=f"x_codes{t}", align_bytes=64)
+            x_scales = keep.tile([P, P], U8, name=f"x_scales{t}", align_bytes=64)
+            nc.vector.quantize_mx(out=x_codes[:].bitcast(E4M3X4), scales=x_scales[:], in_=x_grp[:])
             acc = psum.tile([P, I], F32, name=f"acc{t}")
             nc.tensor.matmul_mx(
                 out=acc[:],
@@ -113,16 +106,15 @@ def tile_list_wgrad_lists_on_both_sides_pl_kernel(tc, xt, gj, mom, offs, offs2, 
                 start=True,
                 stop=True,
             )
-            w_bank.append(acc)
+            return acc
+
+        w_bank = [product(t) for t in range(PACK)]
 
         y = keep.tile([P, PACK, I], F32, name="y")
         y_codes = keep.tile([P, I], U32, name="y_codes", align_bytes=64)
         y_scales = keep.tile([P, I], U8, name="y_scales", align_bytes=64)
         words_out = out_1[0].rearrange("p c r -> p (c r)").bitcast(I32)
         scales_out = out_2[0].bitcast(I32)
-
-        def cols(c, width=CHUNK):
-            return slice(c * width, (c + 1) * width)
 
         def listed_mom(t, c):
             return m_win[t][:].indirect(feat_list[:, cols(c, CHUNK // PER_COL)])
@@ -151,16 +143,15 @@ def tile_list_wgrad_lists_on_both_sides_pl_kernel(tc, xt, gj, mom, offs, offs2, 
             )
 
         y_grp = [keep.tile([P, HALF, PACK], BF16, name=f"y_grp{h}", align_bytes=64) for h in range(2)]
-        for t in range(2):
-            finish_rows(t, (0, 2))
-        nc.sync.dma_start(y_rows[:, 0:2, :], y[:, 0:2, :])
+        finish_rows(0, (3,))
+        finish_rows(1, (0, 2))
         for c in range(CHUNKS):
             round_pair(nc.vector.tensor_copy, 0, c)
         last = PACK - 1
         w_last = keep.tile([P, HALF], F32, name="w_last", tag="d1")
         nc.vector.tensor_scalar_mul(w_last[:], w_bank[last][:, 0:HALF], W_GAIN / MOM_GAIN)
         finish_rows(2, (3,))
-        nc.sync.dma_start(y_rows[:, 2, :], y[:, 2, :])
+        nc.sync.dma_start(y_rows[:, 0:last, :], y[:, 0:last, :])
 
         d = keep.tile([P, I], F32, name="d_last")
         pick = keep.tile([P, I], F32, name="pick_last")

from contextlib import ExitStack

import concourse.mybir as mybir
from concourse.masks import make_identity

K, T, J, N, I = 512, 2048, 512, 2048, 512
FLOPS = 2 * K * J * I

F32 = mybir.dt.float32
BF16 = mybir.dt.bfloat16
U32 = mybir.dt.uint32
U16 = mybir.dt.uint16
I32 = mybir.dt.int32
U8 = mybir.dt.uint8
E4M3X4 = mybir.dt.float8_e4m3fn_x4
E5M2X4 = mybir.dt.float8_e5m2_x4
ACT = mybir.ActivationFunctionType
ALU = mybir.AluOpType

P = 128
PACK = 4
PER_COL = 16
W_GAIN = 0.04
MOM_GAIN = 0.9
HALF = I // 2
CHUNKS = 4
CHUNK = I // CHUNKS


def tile_list_wgrad_lists_on_both_sides_pl_kernel(tc, xt, gj, mom, offs, offs2, out_0, out_1, out_2):
    nc = tc.nc
    with ExitStack() as ctx:
        lists = ctx.enter_context(tc.tile_pool(name="lists", bufs=1))
        keep = ctx.enter_context(tc.tile_pool(name="keep", bufs=1))
        psum = ctx.enter_context(tc.psum_pool(name="psum", bufs=1))

        tok_list = lists.tile([P, J // PER_COL], U16, name="tok_list")
        feat_list = lists.tile([P, I // PER_COL], U16, name="feat_list")

        xt_rows = xt.rearrange("(p t) c -> p t c", t=PACK)
        gj_rows = gj.rearrange("(p t) c -> p t c", t=PACK)
        mom_rows = mom.rearrange("(p t) c -> p t c", t=PACK)
        y_rows = out_0.rearrange("(p t) c -> p t c", t=PACK)

        g_two = [keep.tile([P, 2, N], F32, name=f"g_two{a}") for a in range(2)]
        x_win = [keep.tile([P, T], F32, name=f"x_win{t}") for t in range(PACK)]
        m_win = [keep.tile([P, N], F32, name=f"m_win{t}") for t in range(PACK)]

        nc.sync.dma_start(g_two[0][:], gj_rows[:, 0:2, :])
        nc.sync.dma_start(feat_list[:], offs2)
        nc.sync.dma_start(tok_list[:], offs)
        nc.sync.dma_start(g_two[1][:], gj_rows[:, 2:4, :])
        for t in range(PACK):
            nc.sync.dma_start(x_win[t][:], xt_rows[:, t, :])
        for t in range(PACK):
            nc.sync.dma_start(m_win[t][:], mom_rows[:, t, :])

        ident = keep.tile([P, P], F32, name="ident")
        make_identity(nc, ident[:])

        def cols(c, width=CHUNK):
            return slice(c * width, (c + 1) * width)

        def gather(on_vector, dst, listed):
            if on_vector:
                nc.vector.tensor_copy(dst, listed)
            else:
                nc.scalar.activation(dst, listed, ACT.Copy)

        g_grp = keep.tile([P, I, PACK], BF16, name="g_grp", align_bytes=64)
        for a in range(2):
            g_pick = keep.tile([P, I], F32, name=f"g_pick{a}")
            nc.scalar.activation(g_pick[:], g_two[a][:, 1, :].indirect(feat_list[:]), ACT.Copy)
            nc.vector.tensor_copy(g_grp[:, :, 2 * a], g_two[a][:, 0, :].indirect(feat_list[:]))
            nc.vector.tensor_copy(g_grp[:, :, 2 * a + 1], g_pick[:])
        g_codes = keep.tile([P, I], U32, name="g_codes", align_bytes=64)
        g_scales = keep.tile([P, I], U8, name="g_scales", align_bytes=64)
        nc.vector.quantize_mx(
            out=g_codes[:].bitcast(E5M2X4),
            scales=g_scales[:],
            in_=g_grp[:].rearrange("p c t -> p (c t)"),
        )

        def product(t):
            x_pick = keep.tile([P, J], BF16, name=f"x_pick{t}")
            nc.scalar.activation(x_pick[:], x_win[t][:].indirect(tok_list[:]), ACT.Copy)
            words = x_pick[:].bitcast(F32)
            turned = psum.tile([P, 2, P], F32, name=f"turned{t}")
            for u in range(2):
                nc.tensor.transpose(turned[:, u, :], words[:, u : J // 2 : 2], ident[:])
            x_grp = keep.tile([P, P * PACK], BF16, name=f"x_grp{t}", align_bytes=64)
            nc.vector.tensor_copy(
                x_grp[:].bitcast(F32).rearrange("p (q u) -> p q u", u=2),
                turned[:].rearrange("p u q -> p q u"),
            )
            x_codes = keep.tile([P, P], U32, name=f"x_codes{t}", align_bytes=64)
            x_scales = keep.tile([P, P], U8, name=f"x_scales{t}", align_bytes=64)
            nc.vector.quantize_mx(out=x_codes[:].bitcast(E4M3X4), scales=x_scales[:], in_=x_grp[:])
            acc = psum.tile([P, I], F32, name=f"acc{t}")
            nc.tensor.matmul_mx(
                out=acc[:],
                lhsT=x_codes[:].bitcast(E4M3X4),
                lhsT_scale=x_scales[:],
                rhs=g_codes[:].bitcast(E5M2X4),
                rhs_scale=g_scales[:],
                start=True,
                stop=True,
            )
            return acc

        w_bank = [product(t) for t in range(PACK)]

        y = keep.tile([P, PACK, I], F32, name="y")
        y_codes = keep.tile([P, I], U32, name="y_codes", align_bytes=64)
        y_scales = keep.tile([P, I], U8, name="y_scales", align_bytes=64)
        words_out = out_1[0].rearrange("p c r -> p (c r)").bitcast(I32)
        scales_out = out_2[0].bitcast(I32)

        def listed_mom(t, c):
            return m_win[t][:].indirect(feat_list[:, cols(c, CHUNK // PER_COL)])

        def add_product(d, t, c, pick):
            nc.vector.scalar_tensor_tensor(
                d[:, cols(c)], w_bank[t][:, cols(c)], W_GAIN / MOM_GAIN, pick[:, cols(c)], ALU.mult, ALU.add
            )

        def squash(d, t, c):
            nc.scalar.activation(y[:, t, cols(c)], d[:, cols(c)], ACT.Tanh, scale=MOM_GAIN)

        def finish_rows(t, vector_chunks):
            pick = keep.tile([P, I], F32, name=f"pick{t}")
            for c in range(CHUNKS):
                gather(c in vector_chunks, pick[:, cols(c)], listed_mom(t, c))
            d = keep.tile([P, I], F32, name=f"d{t}", tag=f"d{t}")
            for c in range(CHUNKS):
                add_product(d, t, c, pick)
                squash(d, t, c)

        def round_pair(copy, first, c):
            copy(
                y_grp[c // 2][:, cols(c % 2), first : first + 2],
                y[:, first : first + 2, cols(c)].rearrange("p t c -> p c t"),
            )

        y_grp = [keep.tile([P, HALF, PACK], BF16, name=f"y_grp{h}", align_bytes=64) for h in range(2)]
        finish_rows(0, (3,))
        finish_rows(1, (0, 2))
        for c in range(CHUNKS):
            round_pair(nc.vector.tensor_copy, 0, c)
        last = PACK - 1
        w_last = keep.tile([P, HALF], F32, name="w_last", tag="d1")
        nc.vector.tensor_scalar_mul(w_last[:], w_bank[last][:, 0:HALF], W_GAIN / MOM_GAIN)
        finish_rows(2, (3,))
        nc.sync.dma_start(y_rows[:, 0:last, :], y[:, 0:last, :])

        d = keep.tile([P, I], F32, name="d_last")
        pick = keep.tile([P, I], F32, name="pick_last")
        for c in range(2):
            nc.vector.tensor_tensor(d[:, cols(c)], listed_mom(last, c), w_last[:, cols(c)], ALU.add)
        for c in range(2, CHUNKS):
            gather(False, pick[:, cols(c)], listed_mom(last, c))
        for c in range(2, CHUNKS):
            add_product(d, last, c, pick)
        for c in range(CHUNKS):
            squash(d, last, c)
        nc.sync.dma_start(y_rows[:, last, :], y[:, last, :])
        for c in range(CHUNKS):
            round_pair(nc.vector.tensor_copy if c < CHUNKS - 1 else nc.scalar.copy, 2, c)
        for h in range(2):
            nc.vector.quantize_mx(
                out=y_codes[:, cols(h, HALF)].bitcast(E4M3X4),
                scales=y_scales[:, cols(h, HALF)],
                in_=y_grp[h][:].rearrange("p c t -> p (c t)"),
            )
            nc.sync.dma_start(words_out[:, cols(h, HALF)], y_codes[:, cols(h, HALF)].bitcast(I32))
        for q in range(4):
            queue = nc.scalar if q % 2 == 0 else nc.sync
            queue.dma_start(scales_out[4 * q : 4 * q + 4, :], y_scales[32 * q : 32 * q + 4, :].bitcast(I32))
